import numpy as np
import ml_dtypes


def mxq(x, axis, fmt="e4m3"):
    dtype, down = {"e4m3": (ml_dtypes.float8_e4m3fn, 7), "e5m2": (ml_dtypes.float8_e5m2, 14)}[fmt]
    v = np.moveaxis(np.asarray(x, np.float32).astype(ml_dtypes.bfloat16).astype(np.float64), axis, -1)
    blocks = v.reshape(v.shape[:-1] + (-1, 32))
    amax = np.abs(blocks).max(-1, keepdims=True)
    byte = np.maximum(np.where(amax > 0, np.frexp(amax)[1] - 1 + 127, 0) - down, 1)
    scale = np.exp2(byte - 127.0)
    codes = (blocks / scale).astype(np.float32).astype(dtype).astype(np.float64)
    return np.moveaxis((codes * scale).reshape(v.shape), -1, axis)


WIDE = False


def mx_kscale(k):
    if not WIDE:
        return np.ones(k)
    levels = np.array([10, -10, 5, -5, 0])
    if k % 512:
        return np.exp2(np.random.permutation(np.resize(levels, k // 32))).repeat(32)
    a = np.empty((k // 512, 16))
    for p in range(k // 512):
        a[p, :8] = np.random.permutation(np.resize(levels, 8))
        for g in range(8):
            far = levels[np.abs(levels - a[p, g]) >= 10]
            a[p, g + 8] = far[np.random.randint(len(far))]
    return np.exp2(a.ravel()).repeat(32)


def f64(x):
    return np.asarray(x).astype(np.float64)


def striped(idx):
    return np.tile(idx.reshape(-1, 16).T, (8, 1)).astype(np.uint16)


def unstriped(offs):
    return offs[:16].T.reshape(-1).astype(np.int64)


E2M1 = np.array([0.0, 0.5, 1.0, 1.5, 2.0, 3.0, 4.0, 6.0, -0.0, -0.5, -1.0, -1.5, -2.0, -3.0, -4.0, -6.0])


def pack_weight(w, fmt):
    k, n = w.shape
    w = f64(np.asarray(w, np.float32).astype(ml_dtypes.bfloat16)).reshape(k // 32, 32, n)
    amax = np.abs(w).max(1)
    if fmt == "e4m3":
        byte = np.frexp(amax)[1] - 1 + 127 - 7
    else:
        mant, ex = np.frexp(amax / 6.0)
        byte = np.where(mant > 0.5, ex, ex - 1) + 127
    byte = np.clip(np.where(amax > 0, byte, 1), 1, 254)
    scaled = (w * np.exp2(127.0 - byte)[:, None, :]).reshape(k, n).astype(np.float32)
    by_word = np.ascontiguousarray(scaled.reshape(k // 512, 128, 4, n).transpose(0, 1, 3, 2))
    if fmt == "e4m3":
        words = by_word.astype(ml_dtypes.float8_e4m3fn).view(np.uint8)
    else:
        c = by_word.astype(ml_dtypes.float4_e2m1fn).view(np.uint8) & 0xF
        words = (c[..., 0::2] | (c[..., 1::2] << 4)).reshape(k // 512, 128, 2 * n)
    return np.ascontiguousarray(words), np.ascontiguousarray(byte.astype(np.uint8).reshape(k // 512, 16, n))


def unpack_weight(words, scales, fmt):
    g, _, n = scales.shape
    words = np.ascontiguousarray(words).reshape(g, 128, n, -1)
    if fmt == "e4m3":
        vals = words.view(ml_dtypes.float8_e4m3fn).astype(np.float64)
    else:
        nib = np.empty((g, 128, n, 4), np.uint8)
        nib[..., 0::2] = words & 0xF
        nib[..., 1::2] = words >> 4
        vals = E2M1[nib]
    vals = vals * np.repeat(np.exp2(scales.astype(np.float64) - 127.0), 8, axis=1)[..., None]
    return vals.transpose(0, 1, 3, 2).reshape(g * 512, n)


def gelu(v):
    return 0.5 * v * (1.0 + np.tanh(np.sqrt(2.0 / np.pi) * (v + 0.044715 * v**3)))


def twice(P):
    return np.random.permutation(np.repeat(np.arange(P), 2))


K, H, T, S, P = 512, 1024, 2048, 1024, 512

def setup_inputs():
    n = np.random.standard_normal
    s = mx_kscale(K)[:, None]
    u = mx_kscale(H)[:, None]
    d = {}
    d["tab_words"], d["tab_scales"] = pack_weight(n((K, T)) * s, "e4m3")
    d["offs"] = striped(np.random.permutation(T)[:S])
    d["pos1"] = striped(np.random.permutation(S)[:P])
    d["pos2"] = striped(np.random.permutation(S)[:P])
    d["pos3"] = striped(twice(P))
    d["wa"] = (n((K, H)) / K**0.5 / s * u.T).astype(np.float32)
    d["wb_words"], d["wb_scales"] = pack_weight(n((K, H)) / K**0.5 / s * u.T, "e2m1")
    d["gp"] = (np.exp(0.3 * n(H)) / u[:, 0]).astype(np.float32)
    d["wy_words"], d["wy_scales"] = pack_weight(n((H, H)) / H**0.5 / u, "e4m3")
    d["gh"] = (np.exp(0.3 * n(H)) / u[:, 0]).astype(np.float32)
    return d

def reference(tab_words, tab_scales, offs, pos1, pos2, pos3, wa, wb_words, wb_scales, gp, wy_words, wy_scales, gh):
    v = unpack_weight(tab_words, tab_scales, "e4m3")[:, unstriped(offs)]
    wb = unpack_weight(wb_words, wb_scales, "e2m1")
    wy = unpack_weight(wy_words, wy_scales, "e4m3")
    ha = mxq(f64(wa), 0, "e4m3").T @ v
    hb = wb.T @ v
    h = np.minimum(ha, hb)
    x = h[:, unstriped(pos1)] * h[:, unstriped(pos2)] * f64(gp)[:, None]
    y = wy.T @ mxq(x, 0, "e4m3")
    e = f64(gh)[:, None] * h
    return y[:, unstriped(pos3)] / (1.0 + np.square(e))

@@ -1,0 +1,321 @@
+from contextlib import ExitStack
+
+import concourse.mybir as mybir
+
+K, H, T, S, L = 512, 1024, 2048, 1024, 512
+FLOPS = 2 * (2 * K * H * S + H * H * L)
+
+F32 = mybir.dt.float32
+BF16 = mybir.dt.bfloat16
+I32 = mybir.dt.int32
+U32 = mybir.dt.uint32
+U16 = mybir.dt.uint16
+U8 = mybir.dt.uint8
+FP8X4 = mybir.dt.float8_e4m3fn_x4
+FP4X4 = mybir.dt.float4_e2m1fn_x4
+MULT = mybir.AluOpType.mult
+MIN = mybir.AluOpType.min
+ACT = mybir.ActivationFunctionType
+
+P = 128
+PACK = 4
+GROUP = P * PACK
+GROUPS = H // GROUP
+TILES = H // P
+BANK = 512
+
+
+def tile_list_rink_loop_features_kernel(
+    tc, tab_words, tab_scales, offs, pos1, pos2, pos3, wa, wb_words, wb_scales, gp, wy_words, wy_scales, gh, out
+):
+    nc = tc.nc
+    with ExitStack() as ctx:
+        keep = ctx.enter_context(tc.tile_pool(name="keep", bufs=1))
+        ring = ctx.enter_context(tc.tile_pool(name="ring", bufs=2))
+        outp = ctx.enter_context(tc.tile_pool(name="outp", bufs=3))
+        psum = ctx.enter_context(tc.psum_pool(name="psum", bufs=1))
+
+        def kept(name, shape, dtype):
+            return keep.tile(shape, dtype, name=name, align_bytes=64)
+
+        offs_t = kept("offs_t", [P, S // 16], U16)
+        pos1_t = kept("pos1_t", [P, L // 16], U16)
+        pos2_t = kept("pos2_t", [P, L // 16], U16)
+        pos3_t = kept("pos3_t", [P, S // 16], U16)
+        tabw = kept("tabw", [P, T], I32)
+        tabs = kept("tabs", [P, T], U8)
+        vw = kept("vw", [P, S], U32)
+        vs = kept("vs", [P, S], U8)
+        wa_raw = {}
+        wa_bf = [kept("wa_bf%d" % a, [P, PACK, P, PACK], BF16) for a in range(GROUPS)]
+        wa_w = [kept("wa_w%d" % a, [P, GROUP], U32) for a in range(GROUPS)]
+        wa_s = [kept("wa_s%d" % a, [P, GROUP], U8) for a in range(GROUPS)]
+        wb_raw = kept("wb_raw", [P, 2 * H], U8)
+        bs_raw = kept("bs_raw", [P, H], U8)
+        ys_raw = kept("ys_raw", [P, H], U8)
+        late = {}
+        wy_w = [kept("wy_w%d" % a, [P, H], I32) for a in range(GROUPS)]
+        gp_t = kept("gp_t", [P, GROUPS, PACK], F32)
+        gh_t = kept("gh_t", [P, GROUPS, PACK], F32)
+        gh2 = kept("gh2", [P, TILES], F32)
+        gp_b = [kept("gp_b%d" % n, [P, L], F32) for n in range(TILES)]
+        h = [kept("h%d" % n, [P, S], F32) for n in range(TILES)]
+        yh = [kept("yh%d" % n, [P, L + S], F32) for n in range(TILES)]
+        x_raw = [kept("x_raw%d" % a, [P, PACK, L], F32) for a in range(GROUPS)]
+        spent = x_raw[1][:].rearrange("p t m -> p (t m)")
+        d = [
+            spent[:, S * (n - 4) : S * (n - 3)] if n in (4, 5) else kept("d%d" % n, [P, S], F32)[:] for n in range(TILES)
+        ]
+        x_bf = [kept("x_bf%d" % a, [P, L, PACK], BF16) for a in range(GROUPS)]
+        x_w = [kept("x_w%d" % a, [P, L], U32) for a in range(GROUPS)]
+        x_s = [kept("x_s%d" % a, [P, L], U8) for a in range(GROUPS)]
+        warm = kept("warm", [P, 8], F32)
+
+        nc.gpsimd.dma_start(gh_t[:], gh.rearrange("(a p t) -> p a t", p=P, t=PACK))
+        nc.vector.memset(warm[:], 1.0)
+        nc.vector.memset(ys_raw[:].bitcast(I32), 0)
+        nc.scalar.activation(warm[:, 0:1], warm[:, 1:2], ACT.Abs_reciprocal_sqrt)
+
+        def load_plane(plane, rows):
+            words = rows.shape[1] // 4
+            for q in range(4):
+                nc.sync.dma_start(
+                    plane[32 * q : 32 * q + 32, :].bitcast(I32),
+                    rows[4 * q : 4 * q + 4, :].bitcast(I32).unsqueeze(0).to_broadcast([8, 4, words]),
+                )
+
+        wa_v = wa.rearrange("(p j) c -> p j c", j=PACK)
+
+        def load_wa(a, u):
+            wa_raw[a, u] = kept("wa_raw%d" % u, [P, PACK, GROUP // 2], F32)
+            nc.sync.dma_start(wa_raw[a, u][:], wa_v[:, :, GROUP * a + 256 * u : GROUP * a + 256 * (u + 1)])
+
+        nc.sync.dma_start(offs_t[:], offs)
+        nc.sync.dma_start(gp_t[:], gp.rearrange("(a p t) -> p a t", p=P, t=PACK))
+        load_plane(tabs, tab_scales[0])
+        nc.sync.dma_start(tabw[:], tab_words[0].rearrange("p t i -> p (t i)").bitcast(I32))
+        load_wa(0, 0)
+        load_wa(0, 1)
+        load_plane(bs_raw, wb_scales[0])
+        nc.sync.dma_start(wb_raw[:].bitcast(I32), wb_words[0].bitcast(I32))
+        nc.sync.dma_start(pos1_t[:], pos1)
+        nc.sync.dma_start(pos2_t[:], pos2)
+        nc.sync.dma_start(pos3_t[:], pos3)
+        for q in range(4):
+            nc.sync.dma_start(ys_raw[32 * q : 32 * q + 8, :].bitcast(I32), wy_scales[:, 4 * q : 4 * q + 4, :].bitcast(I32))
+
+        def cast_wa(a, u):
+            nc.scalar.copy(
+                wa_bf[a][:, :, 64 * u : 64 * (u + 1), :].rearrange("p t m j -> p m t j"),
+                wa_raw[a, u][:].rearrange("p j (m t) -> p m t j", t=PACK),
+            )
+
+        def quant_wa(a):
+            nc.vector.quantize_mx(
+                out=wa_w[a][:].bitcast(FP8X4), scales=wa_s[a][:], in_=wa_bf[a][:].rearrange("p t m j -> p (t m j)")
+            )
+
+        banks = {}
+
+        def first_products(n):
+            a, t = divmod(n, PACK)
+            cols = slice(P * t, P * (t + 1))
+            for u in range(2):
+                js = slice(BANK * u, BANK * (u + 1))
+                pb = psum.tile([P, BANK], F32, name="bank%d" % ((4 * n + u) % 8))
+                nc.tensor.matmul_mx(
+                    out=pb[:],
+                    lhsT=wb_w[:, 2 * P * n : 2 * P * (n + 1)].bitcast(FP4X4),
+                    lhsT_scale=bs[:, P * n : P * (n + 1)],
+                    rhs=vw[:, js].bitcast(FP8X4),
+                    rhs_scale=vs[:, js],
+                    start=True,
+                    stop=True,
+                )
+                banks["b", n, u] = pb
+            for u in range(2):
+                js = slice(BANK * u, BANK * (u + 1))
+                pa = psum.tile([P, BANK], F32, name="bank%d" % ((4 * n + 2 + u) % 8))
+                nc.tensor.matmul_mx(
+                    out=pa[:],
+                    lhsT=wa_w[a][:, cols].bitcast(FP8X4),
+                    lhsT_scale=wa_s[a][:, cols],
+                    rhs=vw[:, js].bitcast(FP8X4),
+                    rhs_scale=vs[:, js],
+                    start=True,
+                    stop=True,
+                )
+                banks["a", n, u] = pa
+
+        def copy_hb(n):
+            for u in range(2):
+                nc.scalar.copy(yh[n][:, L + BANK * u : L + BANK * (u + 1)], banks["b", n, u][:])
+
+        def minimum(n):
+            for u in range(2):
+                js = slice(BANK * u, BANK * (u + 1))
+                nc.vector.tensor_tensor(h[n][:, js], banks["a", n, u][:], yh[n][:, L + BANK * u : L + BANK * (u + 1)], MIN)
+
+        firsts = {}
+
+        def pick1(n):
+            a, t = divmod(n, PACK)
+            nc.scalar.copy(gp_b[n][:], gp_t[:, a, t : t + 1].to_broadcast([P, L]))
+            g1 = ring.tile([P, L], F32, name="g1")
+            nc.vector.tensor_tensor(g1[:], h[n][:].indirect(pos1_t[:]), gp_b[n][:], MULT)
+            firsts[n] = g1
+
+        def pick2(n, lo, hi):
+            a, t = divmod(n, PACK)
+            nc.vector.tensor_tensor(
+                x_raw[a][:, t, lo:hi], h[n][:].indirect(pos2_t[:, lo // 16 : hi // 16]), firsts[n][:, lo:hi], MULT
+            )
+
+        def weave_scalar(a, lo, hi):
+            nc.scalar.copy(x_bf[a][:, lo:hi, :], x_raw[a][:, :, lo:hi].rearrange("p t m -> p m t"))
+
+        def weave_vector(a, lo, hi):
+            nc.vector.tensor_copy(x_bf[a][:, lo:hi, :], x_raw[a][:, :, lo:hi].rearrange("p t m -> p m t"))
+
+        def quant_x(a, lo, hi):
+            nc.vector.quantize_mx(
+                out=x_w[a][:, lo:hi].bitcast(FP8X4),
+                scales=x_s[a][:, lo:hi],
+                in_=x_bf[a][:, lo:hi, :].rearrange("p m t -> p (m t)"),
+            )
+
+        def damp(n, step):
+            a, t = divmod(n, PACK)
+            if step == 0:
+                nc.scalar.activation(d[n], h[n][:], ACT.Square, scale=gh_t[:, a, t : t + 1])
+            elif step == 1:
+                nc.scalar.activation(d[n], d[n], ACT.Abs_reciprocal_sqrt, bias=1.0)
+            else:
+                nc.scalar.activation(d[n], d[n], ACT.Square)
+
+        def damp0_vector(n):
+            nc.vector.scalar_tensor_tensor(d[n], h[n][:], gh2[:, n : n + 1], h[n][:], MULT, MULT)
+
+        ybanks = {}
+
+        def second_product(n, a):
+            cols = slice(P * n, P * (n + 1))
+            if a == 0:
+                ybanks[n] = psum.tile([P, BANK], F32, name="bank%d" % n)
+            nc.tensor.matmul_mx(
+                out=ybanks[n][:],
+                lhsT=wy_w[a][:, cols].bitcast(FP8X4),
+                lhsT_scale=late["ys"][4 * a :, cols],
+                rhs=x_w[a][:].bitcast(FP8X4),
+                rhs_scale=x_s[a][:],
+                start=(a == 0),
+                stop=(a == GROUPS - 1),
+            )
+
+        def copy_y(n):
+            nc.scalar.copy(yh[n][:, 0:L], ybanks[n][:])
+
+        out_v = out.rearrange("(a p t) j -> a t p j", p=P, t=PACK)
+
+        def finish(n, pieces):
+            a, t = divmod(n, PACK)
+            width = S // pieces
+            for u in range(pieces):
+                res = outp.tile([P, width], F32, name="res")
+                js = slice(width * u, width * (u + 1))
+                nc.vector.tensor_tensor(
+                    res[:], yh[n][:].indirect(pos3_t[:, width * u // 16 : width * (u + 1) // 16]), d[n][:, js], MULT
+                )
+                nc.sync.dma_start(out_v[a, t, :, js], res[:])
+
+        nc.vector.tensor_copy(vs[:], tabs[:].indirect(offs_t[:]))
+        nc.vector.tensor_copy(vw[:], tabw[:].bitcast(U32).indirect(offs_t[:]))
+        dealt = kept("tabw", [P, 3 * H], U8)
+        wb_w = dealt[:, : 2 * H]
+        bs = dealt[:, 2 * H :]
+        cast_wa(0, 0)
+        cast_wa(0, 1)
+        load_wa(1, 0)
+        load_wa(1, 1)
+
+        def load_wy(a):
+            late["wy_raw", a] = kept("wa_raw%d" % a, [P, H], I32)
+            nc.sync.dma_start(late["wy_raw", a][:], wy_words[a].rearrange("p c i -> p (c i)").bitcast(I32))
+
+        def deal_ys():
+            late["ys"] = kept("wa_bf1", [P, H], U8)
+            deal_plane(late["ys"][:], ys_raw)
+
+        def deal_plane(plane, raw):
+            nc.vector.tensor_copy(
+                plane.rearrange("p (a t m) -> p a t m", a=GROUPS, t=PACK),
+                raw[:].rearrange("p (a m t) -> p a t m", a=GROUPS, t=PACK),
+            )
+
+        def deal_wb(a):
+            nc.vector.tensor_copy(
+                wb_w.bitcast(U16)[:, GROUP * a : GROUP * (a + 1)].rearrange("p (t m) -> p m t", t=PACK),
+                wb_raw[:].bitcast(U16)[:, GROUP * a : GROUP * (a + 1)].rearrange("p (m t) -> p m t", t=PACK),
+            )
+
+        deal_wb(0)
+        deal_plane(bs, bs_raw)
+        gh_flat = gh_t[:].rearrange("p a t -> p (a t)")
+        nc.gpsimd.tensor_tensor(gh2[:], gh_flat, gh_flat, MULT)
+        quant_wa(0)
+        first_products(0)
+        deal_wb(1)
+        copy_hb(0)
+
+        def deal_wy(a):
+            nc.vector.tensor_copy(
+                wy_w[a][:].rearrange("p (g t m) -> p g m t", g=GROUPS, t=PACK),
+                late["wy_raw", a][:].rearrange("p (g m t) -> p g m t", g=GROUPS, t=PACK),
+            )
+
+        extra = {
+            0: [lambda: cast_wa(1, 0), lambda: load_wy(0)],
+            1: [lambda: cast_wa(1, 1), lambda: load_wy(1), lambda: damp(0, 0)],
+            2: [lambda: quant_wa(1), lambda: damp(0, 1), lambda: damp(0, 2), deal_ys],
+            3: [lambda: damp(1, 0), lambda: damp(1, 1), lambda: deal_wy(0)],
+            4: [lambda: weave_scalar(0, 0, 256), lambda: weave_scalar(0, 256, 512), lambda: deal_wy(1)],
+            5: [lambda: damp(1, 2), lambda: damp(2, 0), lambda: quant_x(0, 0, 512)],
+            6: [lambda: damp(2, 1), lambda: damp(2, 2)],
+            7: [lambda: damp(3, 0), lambda: damp(3, 1)],
+        }
+        for n in range(TILES):
+            if n == 2:
+                extra[n][0]()
+            if n + 1 < TILES:
+                first_products(n + 1)
+            minimum(n)
+            if n + 1 < TILES:
+                copy_hb(n + 1)
+            pick1(n)
+            if n + 1 < TILES:
+                pick2(n, 0, L)
+                for f in extra[n][1 if n == 2 else 0 :]:
+                    f()
+        last = TILES - 1
+        damp(3, 0)
+        pick2(last, 0, 256)
+        weave_scalar(1, 0, 256)
+        for n in range(TILES):
+            second_product(n, 0)
+        pick2(last, 256, 512)
+        weave_vector(1, 256, 512)
+        quant_x(1, 0, 256)
+        quant_x(1, 256, 512)
+        for n in range(TILES):
+            second_product(n, 1)
+        damp(3, 1)
+        damp0_vector(4)
+        damp0_vector(5)
+        rest = [(3, 2), (4, 1), (4, 2), (5, 1), (5, 2), (6, 0), (6, 1), (6, 2), (7, 0), (7, 1), (7, 2)]
+        copy_y(0)
+        for n in range(TILES):
+            if n < last:
+                copy_y(n + 1)
+            for item in rest[2 * n : 2 * n + 2]:
+                damp(*item)
+            finish(n, 1 if n < last else 4)

@@ -23,6 +23,8 @@ GROUP = P * PACK
 GROUPS = H // GROUP
 TILES = H // P
 BANK = 512
+WA_PIECES = ((0, 256), (256, 384), (384, 512))
+LAST_PIECES = (0, 512, 768, 896, 1024)
 
 
 def tile_list_rink_loop_features_kernel(
@@ -32,7 +34,7 @@ def tile_list_rink_loop_features_kernel(
     with ExitStack() as ctx:
         keep = ctx.enter_context(tc.tile_pool(name="keep", bufs=1))
         ring = ctx.enter_context(tc.tile_pool(name="ring", bufs=2))
-        outp = ctx.enter_context(tc.tile_pool(name="outp", bufs=3))
+        outp = ctx.enter_context(tc.tile_pool(name="outp", bufs=5))
         psum = ctx.enter_context(tc.psum_pool(name="psum", bufs=1))
 
         def kept(name, shape, dtype):
@@ -54,7 +56,6 @@ def tile_list_rink_loop_features_kernel(
         bs_raw = kept("bs_raw", [P, H], U8)
         ys_raw = kept("ys_raw", [P, H], U8)
         late = {}
-        wy_w = [kept("wy_w%d" % a, [P, H], I32) for a in range(GROUPS)]
         gp_t = kept("gp_t", [P, GROUPS, PACK], F32)
         gh_t = kept("gh_t", [P, GROUPS, PACK], F32)
         gh2 = kept("gh2", [P, TILES], F32)
@@ -62,10 +63,7 @@ def tile_list_rink_loop_features_kernel(
         h = [kept("h%d" % n, [P, S], F32) for n in range(TILES)]
         yh = [kept("yh%d" % n, [P, L + S], F32) for n in range(TILES)]
         x_raw = [kept("x_raw%d" % a, [P, PACK, L], F32) for a in range(GROUPS)]
-        spent = x_raw[1][:].rearrange("p t m -> p (t m)")
-        d = [
-            spent[:, S * (n - 4) : S * (n - 3)] if n in (4, 5) else kept("d%d" % n, [P, S], F32)[:] for n in range(TILES)
-        ]
+        d = {n: kept("d%d" % n, [P, S], F32)[:] for n in range(TILES) if n != 4}
         x_bf = [kept("x_bf%d" % a, [P, L, PACK], BF16) for a in range(GROUPS)]
         x_w = [kept("x_w%d" % a, [P, L], U32) for a in range(GROUPS)]
         x_s = [kept("x_s%d" % a, [P, L], U8) for a in range(GROUPS)]
@@ -87,8 +85,9 @@ def tile_list_rink_loop_features_kernel(
         wa_v = wa.rearrange("(p j) c -> p j c", j=PACK)
 
         def load_wa(a, u):
-            wa_raw[a, u] = kept("wa_raw%d" % u, [P, PACK, GROUP // 2], F32)
-            nc.sync.dma_start(wa_raw[a, u][:], wa_v[:, :, GROUP * a + 256 * u : GROUP * a + 256 * (u + 1)])
+            lo, hi = WA_PIECES[u]
+            wa_raw[a, u] = kept("wa_raw%d" % u, [P, PACK, hi - lo], F32)
+            nc.sync.dma_start(wa_raw[a, u][:], wa_v[:, :, GROUP * a + lo : GROUP * a + hi])
 
         nc.sync.dma_start(offs_t[:], offs)
         nc.sync.dma_start(gp_t[:], gp.rearrange("(a p t) -> p a t", p=P, t=PACK))
@@ -96,8 +95,9 @@ def tile_list_rink_loop_features_kernel(
         nc.sync.dma_start(tabw[:], tab_words[0].rearrange("p t i -> p (t i)").bitcast(I32))
         load_wa(0, 0)
         load_wa(0, 1)
-        load_plane(bs_raw, wb_scales[0])
+        load_wa(0, 2)
         nc.sync.dma_start(wb_raw[:].bitcast(I32), wb_words[0].bitcast(I32))
+        load_plane(bs_raw, wb_scales[0])
         nc.sync.dma_start(pos1_t[:], pos1)
         nc.sync.dma_start(pos2_t[:], pos2)
         nc.sync.dma_start(pos3_t[:], pos3)
@@ -105,71 +105,67 @@ def tile_list_rink_loop_features_kernel(
             nc.sync.dma_start(ys_raw[32 * q : 32 * q + 8, :].bitcast(I32), wy_scales[:, 4 * q : 4 * q + 4, :].bitcast(I32))
 
         def cast_wa(a, u):
+            lo, hi = WA_PIECES[u]
             nc.scalar.copy(
-                wa_bf[a][:, :, 64 * u : 64 * (u + 1), :].rearrange("p t m j -> p m t j"),
+                wa_bf[a][:, :, lo // PACK : hi // PACK, :].rearrange("p t m j -> p m t j"),
                 wa_raw[a, u][:].rearrange("p j (m t) -> p m t j", t=PACK),
             )
 
-        def quant_wa(a):
+        def quant_wa(a, u):
+            cols = slice(2 * P * u, 2 * P * (u + 1))
             nc.vector.quantize_mx(
-                out=wa_w[a][:].bitcast(FP8X4), scales=wa_s[a][:], in_=wa_bf[a][:].rearrange("p t m j -> p (t m j)")
+                out=wa_w[a][:, cols].bitcast(FP8X4),
+                scales=wa_s[a][:, cols],
+                in_=wa_bf[a][:, 2 * u : 2 * u + 2].rearrange("p t m j -> p (t m j)"),
             )
 
         banks = {}
 
-        def first_products(n):
+        def first_products(n, u):
             a, t = divmod(n, PACK)
             cols = slice(P * t, P * (t + 1))
-            for u in range(2):
-                js = slice(BANK * u, BANK * (u + 1))
-                pb = psum.tile([P, BANK], F32, name="bank%d" % ((4 * n + u) % 8))
-                nc.tensor.matmul_mx(
-                    out=pb[:],
-                    lhsT=wb_w[:, 2 * P * n : 2 * P * (n + 1)].bitcast(FP4X4),
-                    lhsT_scale=bs[:, P * n : P * (n + 1)],
-                    rhs=vw[:, js].bitcast(FP8X4),
-                    rhs_scale=vs[:, js],
-                    start=True,
-                    stop=True,
-                )
-                banks["b", n, u] = pb
-            for u in range(2):
-                js = slice(BANK * u, BANK * (u + 1))
-                pa = psum.tile([P, BANK], F32, name="bank%d" % ((4 * n + 2 + u) % 8))
-                nc.tensor.matmul_mx(
-                    out=pa[:],
-                    lhsT=wa_w[a][:, cols].bitcast(FP8X4),
-                    lhsT_scale=wa_s[a][:, cols],
-                    rhs=vw[:, js].bitcast(FP8X4),
-                    rhs_scale=vs[:, js],
-                    start=True,
-                    stop=True,
-                )
-                banks["a", n, u] = pa
+            js = slice(BANK * u, BANK * (u + 1))
+            pb = psum.tile([P, BANK], F32, name="bank%d" % ((4 * n + u) % 8))
+            nc.tensor.matmul_mx(
+                out=pb[:],
+                lhsT=wb_w[:, 2 * P * n : 2 * P * (n + 1)].bitcast(FP4X4),
+                lhsT_scale=bs[:, P * n : P * (n + 1)],
+                rhs=vw[:, js].bitcast(FP8X4),
+                rhs_scale=vs[:, js],
+                start=True,
+                stop=True,
+            )
+            pa = psum.tile([P, BANK], F32, name="bank%d" % ((4 * n + 2 + u) % 8))
+            nc.tensor.matmul_mx(
+                out=pa[:],
+                lhsT=wa_w[a][:, cols].bitcast(FP8X4),
+                lhsT_scale=wa_s[a][:, cols],
+                rhs=vw[:, js].bitcast(FP8X4),
+                rhs_scale=vs[:, js],
+                start=True,
+                stop=True,
+            )
+            banks[n, u] = (pa, pb)
 
-        def copy_hb(n):
-            for u in range(2):
-                nc.scalar.copy(yh[n][:, L + BANK * u : L + BANK * (u + 1)], banks["b", n, u][:])
+        def copy_hb(n, u):
+            nc.scalar.copy(yh[n][:, L + BANK * u : L + BANK * (u + 1)], banks[n, u][1][:])
 
-        def minimum(n):
-            for u in range(2):
-                js = slice(BANK * u, BANK * (u + 1))
-                nc.vector.tensor_tensor(h[n][:, js], banks["a", n, u][:], yh[n][:, L + BANK * u : L + BANK * (u + 1)], MIN)
+        def minimum(n, u):
+            js = slice(BANK * u, BANK * (u + 1))
+            nc.vector.tensor_tensor(h[n][:, js], banks[n, u][0][:], yh[n][:, L + BANK * u : L + BANK * (u + 1)], MIN)
 
-        firsts = {}
-
-        def pick1(n):
+        def picks(n):
             a, t = divmod(n, PACK)
             nc.scalar.copy(gp_b[n][:], gp_t[:, a, t : t + 1].to_broadcast([P, L]))
             g1 = ring.tile([P, L], F32, name="g1")
-            nc.vector.tensor_tensor(g1[:], h[n][:].indirect(pos1_t[:]), gp_b[n][:], MULT)
-            firsts[n] = g1
-
-        def pick2(n, lo, hi):
-            a, t = divmod(n, PACK)
-            nc.vector.tensor_tensor(
-                x_raw[a][:, t, lo:hi], h[n][:].indirect(pos2_t[:, lo // 16 : hi // 16]), firsts[n][:, lo:hi], MULT
-            )
+            for lo, hi in ((0, 256), (256, 512)):
+                nc.vector.tensor_tensor(
+                    g1[:, lo:hi], h[n][:].indirect(pos1_t[:, lo // 16 : hi // 16]), gp_b[n][:, lo:hi], MULT
+                )
+            for lo, hi in ((0, 256), (256, 512)):
+                nc.vector.tensor_tensor(
+                    x_raw[a][:, t, lo:hi], h[n][:].indirect(pos2_t[:, lo // 16 : hi // 16]), g1[:, lo:hi], MULT
+                )
 
         def weave_scalar(a, lo, hi):
             nc.scalar.copy(x_bf[a][:, lo:hi, :], x_raw[a][:, :, lo:hi].rearrange("p t m -> p m t"))
@@ -199,13 +195,13 @@ def tile_list_rink_loop_features_kernel(
         ybanks = {}
 
         def second_product(n, a):
-            cols = slice(P * n, P * (n + 1))
+            g, t = divmod(n, PACK)
             if a == 0:
                 ybanks[n] = psum.tile([P, BANK], F32, name="bank%d" % n)
             nc.tensor.matmul_mx(
                 out=ybanks[n][:],
-                lhsT=wy_w[a][:, cols].bitcast(FP8X4),
-                lhsT_scale=late["ys"][4 * a :, cols],
+                lhsT=late["wy", g][:, GROUP * a + P * t : GROUP * a + P * (t + 1)].bitcast(FP8X4),
+                lhsT_scale=late["ys", g][4 * a :, P * t : P * (t + 1)],
                 rhs=x_w[a][:].bitcast(FP8X4),
                 rhs_scale=x_s[a][:],
                 start=(a == 0),
@@ -217,105 +213,109 @@ def tile_list_rink_loop_features_kernel(
 
         out_v = out.rearrange("(a p t) j -> a t p j", p=P, t=PACK)
 
-        def finish(n, pieces):
+        def finish(n, cuts):
             a, t = divmod(n, PACK)
-            width = S // pieces
-            for u in range(pieces):
-                res = outp.tile([P, width], F32, name="res")
-                js = slice(width * u, width * (u + 1))
+            for lo, hi in zip(cuts, cuts[1:]):
+                res = outp.tile([P, hi - lo], F32, name="res")
                 nc.vector.tensor_tensor(
-                    res[:], yh[n][:].indirect(pos3_t[:, width * u // 16 : width * (u + 1) // 16]), d[n][:, js], MULT
+                    res[:], yh[n][:].indirect(pos3_t[:, lo // 16 : hi // 16]), d[n][:, lo:hi], MULT
                 )
-                nc.sync.dma_start(out_v[a, t, :, js], res[:])
+                nc.sync.dma_start(out_v[a, t, :, lo:hi], res[:])
 
         nc.vector.tensor_copy(vs[:], tabs[:].indirect(offs_t[:]))
         nc.vector.tensor_copy(vw[:], tabw[:].bitcast(U32).indirect(offs_t[:]))
-        dealt = kept("tabw", [P, 3 * H], U8)
-        wb_w = dealt[:, : 2 * H]
-        bs = dealt[:, 2 * H :]
+        dealt_b = kept("tabw", [P, 3 * H], U8)
+        wb_w = dealt_b[:, : 2 * H]
+        bs = dealt_b[:, 2 * H :]
         cast_wa(0, 0)
         cast_wa(0, 1)
+        cast_wa(0, 2)
         load_wa(1, 0)
         load_wa(1, 1)
+        load_wa(1, 2)
 
         def load_wy(a):
             late["wy_raw", a] = kept("wa_raw%d" % a, [P, H], I32)
             nc.sync.dma_start(late["wy_raw", a][:], wy_words[a].rearrange("p c i -> p (c i)").bitcast(I32))
 
-        def deal_ys():
-            late["ys"] = kept("wa_bf1", [P, H], U8)
-            deal_plane(late["ys"][:], ys_raw)
-
-        def deal_plane(plane, raw):
+        def deal(dealt, raw):
             nc.vector.tensor_copy(
-                plane.rearrange("p (a t m) -> p a t m", a=GROUPS, t=PACK),
-                raw[:].rearrange("p (a m t) -> p a t m", a=GROUPS, t=PACK),
+                dealt.rearrange("p (t m) -> p t m", t=PACK), raw.rearrange("p (m t) -> p t m", t=PACK)
+            )
+
+        def deal_words(dealt, raw):
+            nc.vector.tensor_copy(
+                dealt.rearrange("p (t c i) -> p c t i", t=PACK, i=4), raw.rearrange("p (c i t) -> p c t i", t=PACK, i=4)
             )
 
         def deal_wb(a):
-            nc.vector.tensor_copy(
-                wb_w.bitcast(U16)[:, GROUP * a : GROUP * (a + 1)].rearrange("p (t m) -> p m t", t=PACK),
-                wb_raw[:].bitcast(U16)[:, GROUP * a : GROUP * (a + 1)].rearrange("p (m t) -> p m t", t=PACK),
-            )
+            cols = slice(GROUP * a, GROUP * (a + 1))
+            deal(wb_w.bitcast(U16)[:, cols], wb_raw[:].bitcast(U16)[:, cols])
+            deal(bs[:, cols], bs_raw[:, cols])
+
+        def deal_wy(g, tag):
+            both = kept(tag, [P, GROUPS * GROUP + GROUP // 4], I32)
+            late["wy", g] = both[:, : GROUPS * GROUP]
+            late["ys", g] = both[:, GROUPS * GROUP :].bitcast(U8)
+            cols = slice(GROUP * g, GROUP * (g + 1))
+            for a in range(GROUPS):
+                deal_words(both[:, GROUP * a : GROUP * (a + 1)], late["wy_raw", a][:, cols])
+            deal(late["ys", g], ys_raw[:, cols])
 
         deal_wb(0)
-        deal_plane(bs, bs_raw)
         gh_flat = gh_t[:].rearrange("p a t -> p (a t)")
         nc.gpsimd.tensor_tensor(gh2[:], gh_flat, gh_flat, MULT)
-        quant_wa(0)
-        first_products(0)
+        quant_wa(0, 0)
+        first_products(0, 0)
+        quant_wa(0, 1)
         deal_wb(1)
-        copy_hb(0)
-
-        def deal_wy(a):
-            nc.vector.tensor_copy(
-                wy_w[a][:].rearrange("p (g t m) -> p g m t", g=GROUPS, t=PACK),
-                late["wy_raw", a][:].rearrange("p (g m t) -> p g m t", g=GROUPS, t=PACK),
-            )
+        copy_hb(0, 0)
+        minimum(0, 0)
 
         extra = {
-            0: [lambda: cast_wa(1, 0), lambda: load_wy(0)],
-            1: [lambda: cast_wa(1, 1), lambda: load_wy(1), lambda: damp(0, 0)],
-            2: [lambda: quant_wa(1), lambda: damp(0, 1), lambda: damp(0, 2), deal_ys],
-            3: [lambda: damp(1, 0), lambda: damp(1, 1), lambda: deal_wy(0)],
-            4: [lambda: weave_scalar(0, 0, 256), lambda: weave_scalar(0, 256, 512), lambda: deal_wy(1)],
-            5: [lambda: damp(1, 2), lambda: damp(2, 0), lambda: quant_x(0, 0, 512)],
-            6: [lambda: damp(2, 1), lambda: damp(2, 2)],
-            7: [lambda: damp(3, 0), lambda: damp(3, 1)],
+            0: [lambda: cast_wa(1, 0), lambda: load_wy(0), lambda: cast_wa(1, 1), lambda: load_wy(1), lambda: cast_wa(1, 2)],
+            1: [lambda: damp(0, 0), lambda: damp(0, 1), lambda: quant_wa(1, 0), lambda: quant_wa(1, 1)],
+            2: [lambda: damp(0, 2), lambda: damp(1, 0)],
+            3: [lambda: damp(1, 1), lambda: damp(1, 2), lambda: deal_wy(0, "wa_bf1")],
+            4: [lambda: weave_scalar(0, 0, 256), lambda: weave_scalar(0, 256, 512)],
+            5: [lambda: damp(2, 0), lambda: damp(2, 1), lambda: quant_x(0, 0, 512)],
+            6: [lambda: damp(2, 2), lambda: damp(3, 0), lambda: damp(3, 1)],
+            7: [],
         }
-        for n in range(TILES):
-            if n == 2:
-                extra[n][0]()
-            if n + 1 < TILES:
-                first_products(n + 1)
-            minimum(n)
-            if n + 1 < TILES:
-                copy_hb(n + 1)
-            pick1(n)
-            if n + 1 < TILES:
-                pick2(n, 0, L)
-                for f in extra[n][1 if n == 2 else 0 :]:
-                    f()
         last = TILES - 1
-        damp(3, 0)
-        pick2(last, 0, 256)
-        weave_scalar(1, 0, 256)
         for n in range(TILES):
+            first_products(n, 1)
+            if n < last:
+                first_products(n + 1, 0)
+            copy_hb(n, 1)
+            if n < last:
+                copy_hb(n + 1, 0)
+            minimum(n, 1)
+            if n < last:
+                minimum(n + 1, 0)
+            picks(n)
+            for f in extra[n]:
+                f()
+        weave_scalar(1, 0, 256)
+        for n in range(PACK):
             second_product(n, 0)
-        pick2(last, 256, 512)
         weave_vector(1, 256, 512)
         quant_x(1, 0, 256)
         quant_x(1, 256, 512)
-        for n in range(TILES):
+        for n in range(PACK):
             second_product(n, 1)
-        damp(3, 1)
+        deal_wy(1, "x_raw1")
+        for n in range(PACK, TILES):
+            second_product(n, 0)
+            second_product(n, 1)
+        damp(3, 2)
+        d[4] = kept("x_bf1", [P, S], F32)[:]
         damp0_vector(4)
-        damp0_vector(5)
-        rest = [(3, 2), (4, 1), (4, 2), (5, 1), (5, 2), (6, 0), (6, 1), (6, 2), (7, 0), (7, 1), (7, 2)]
+        rest = [(4, 1), (4, 2)] + [(n, step) for n in range(5, TILES) for step in range(3)]
         copy_y(0)
         for n in range(TILES):
             if n < last:
                 copy_y(n + 1)
             for item in rest[2 * n : 2 * n + 2]:
                 damp(*item)
-            finish(n, 1 if n < last else 4)
+            finish(n, (0, S) if n < last else LAST_PIECES)

@@ -23,7 +23,7 @@ GROUP = P * PACK
 GROUPS = H // GROUP
 TILES = H // P
 BANK = 512
-WA_PIECES = ((0, 256), (256, 384), (384, 512))
+WA_PIECES = ((0, 320), (320, 512))
 LAST_PIECES = (0, 512, 768, 896, 1024)
 
 
@@ -34,7 +34,8 @@ def tile_list_rink_loop_features_kernel(
     with ExitStack() as ctx:
         keep = ctx.enter_context(tc.tile_pool(name="keep", bufs=1))
         ring = ctx.enter_context(tc.tile_pool(name="ring", bufs=2))
-        outp = ctx.enter_context(tc.tile_pool(name="outp", bufs=5))
+        gains = ctx.enter_context(tc.tile_pool(name="gains", bufs=5))
+        outp = ctx.enter_context(tc.tile_pool(name="outp", bufs=6))
         psum = ctx.enter_context(tc.psum_pool(name="psum", bufs=1))
 
         def kept(name, shape, dtype):
@@ -58,26 +59,23 @@ def tile_list_rink_loop_features_kernel(
         late = {}
         gp_t = kept("gp_t", [P, GROUPS, PACK], F32)
         gh_t = kept("gh_t", [P, GROUPS, PACK], F32)
-        gh2 = kept("gh2", [P, TILES], F32)
-        gp_b = [kept("gp_b%d" % n, [P, L], F32) for n in range(TILES)]
         h = [kept("h%d" % n, [P, S], F32) for n in range(TILES)]
-        yh = [kept("yh%d" % n, [P, L + S], F32) for n in range(TILES)]
+        yh = {n: kept("yh%d" % n, [P, L + S], F32) for n in range(2, TILES)}
         x_raw = [kept("x_raw%d" % a, [P, PACK, L], F32) for a in range(GROUPS)]
-        d = {n: kept("d%d" % n, [P, S], F32)[:] for n in range(TILES) if n != 4}
+        d = {n: kept("d%d" % n, [P, S], F32)[:] for n in range(TILES)}
         x_bf = [kept("x_bf%d" % a, [P, L, PACK], BF16) for a in range(GROUPS)]
         x_w = [kept("x_w%d" % a, [P, L], U32) for a in range(GROUPS)]
         x_s = [kept("x_s%d" % a, [P, L], U8) for a in range(GROUPS)]
         warm = kept("warm", [P, 8], F32)
 
-        nc.gpsimd.dma_start(gh_t[:], gh.rearrange("(a p t) -> p a t", p=P, t=PACK))
         nc.vector.memset(warm[:], 1.0)
         nc.vector.memset(ys_raw[:].bitcast(I32), 0)
         nc.scalar.activation(warm[:, 0:1], warm[:, 1:2], ACT.Abs_reciprocal_sqrt)
 
-        def load_plane(plane, rows):
+        def load_plane(queue, plane, rows):
             words = rows.shape[1] // 4
             for q in range(4):
-                nc.sync.dma_start(
+                queue.dma_start(
                     plane[32 * q : 32 * q + 32, :].bitcast(I32),
                     rows[4 * q : 4 * q + 4, :].bitcast(I32).unsqueeze(0).to_broadcast([8, 4, words]),
                 )
@@ -86,29 +84,30 @@ def tile_list_rink_loop_features_kernel(
 
         def load_wa(a, u):
             lo, hi = WA_PIECES[u]
-            wa_raw[a, u] = kept("wa_raw%d" % u, [P, PACK, hi - lo], F32)
+            tag = {(0, 0): "wa_raw0", (0, 1): "yh0", (1, 0): "wa_raw0", (1, 1): "tabs"}[a, u]
+            wa_raw[a, u] = kept(tag, [P, PACK, hi - lo], F32)
             nc.sync.dma_start(wa_raw[a, u][:], wa_v[:, :, GROUP * a + lo : GROUP * a + hi])
 
         nc.sync.dma_start(offs_t[:], offs)
         nc.sync.dma_start(gp_t[:], gp.rearrange("(a p t) -> p a t", p=P, t=PACK))
-        load_plane(tabs, tab_scales[0])
+        load_plane(nc.sync, tabs, tab_scales[0])
         nc.sync.dma_start(tabw[:], tab_words[0].rearrange("p t i -> p (t i)").bitcast(I32))
         load_wa(0, 0)
-        load_wa(0, 1)
-        load_wa(0, 2)
         nc.sync.dma_start(wb_raw[:].bitcast(I32), wb_words[0].bitcast(I32))
-        load_plane(bs_raw, wb_scales[0])
+        load_plane(nc.sync, bs_raw, wb_scales[0])
+        load_wa(0, 1)
         nc.sync.dma_start(pos1_t[:], pos1)
         nc.sync.dma_start(pos2_t[:], pos2)
+        nc.sync.dma_start(gh_t[:], gh.rearrange("(a p t) -> p a t", p=P, t=PACK))
         nc.sync.dma_start(pos3_t[:], pos3)
         for q in range(4):
             nc.sync.dma_start(ys_raw[32 * q : 32 * q + 8, :].bitcast(I32), wy_scales[:, 4 * q : 4 * q + 4, :].bitcast(I32))
 
-        def cast_wa(a, u):
+        def cast_wa(a, u, copy=nc.scalar.copy):
             lo, hi = WA_PIECES[u]
-            nc.scalar.copy(
-                wa_bf[a][:, :, lo // PACK : hi // PACK, :].rearrange("p t m j -> p m t j"),
-                wa_raw[a, u][:].rearrange("p j (m t) -> p m t j", t=PACK),
+            copy(
+                wa_bf[a][:, :, lo // PACK : hi // PACK, :].rearrange("p t m j -> p m j t"),
+                wa_raw[a, u][:].rearrange("p j (m t) -> p m j t", t=PACK),
             )
 
         def quant_wa(a, u):
@@ -125,7 +124,7 @@ def tile_list_rink_loop_features_kernel(
             a, t = divmod(n, PACK)
             cols = slice(P * t, P * (t + 1))
             js = slice(BANK * u, BANK * (u + 1))
-            pb = psum.tile([P, BANK], F32, name="bank%d" % ((4 * n + u) % 8))
+            pb = psum.tile([P, BANK], F32, name="bank%d" % u)
             nc.tensor.matmul_mx(
                 out=pb[:],
                 lhsT=wb_w[:, 2 * P * n : 2 * P * (n + 1)].bitcast(FP4X4),
@@ -135,7 +134,7 @@ def tile_list_rink_loop_features_kernel(
                 start=True,
                 stop=True,
             )
-            pa = psum.tile([P, BANK], F32, name="bank%d" % ((4 * n + 2 + u) % 8))
+            pa = psum.tile([P, BANK], F32, name="bank%d" % (2 + (2 * n + u) % 4))
             nc.tensor.matmul_mx(
                 out=pa[:],
                 lhsT=wa_w[a][:, cols].bitcast(FP8X4),
@@ -156,11 +155,12 @@ def tile_list_rink_loop_features_kernel(
 
         def picks(n):
             a, t = divmod(n, PACK)
-            nc.scalar.copy(gp_b[n][:], gp_t[:, a, t : t + 1].to_broadcast([P, L]))
+            gp_b = gains.tile([P, L], F32, name="gp_b")
+            nc.scalar.copy(gp_b[:], gp_t[:, a, t : t + 1].to_broadcast([P, L]))
             g1 = ring.tile([P, L], F32, name="g1")
             for lo, hi in ((0, 256), (256, 512)):
                 nc.vector.tensor_tensor(
-                    g1[:, lo:hi], h[n][:].indirect(pos1_t[:, lo // 16 : hi // 16]), gp_b[n][:, lo:hi], MULT
+                    g1[:, lo:hi], h[n][:].indirect(pos1_t[:, lo // 16 : hi // 16]), gp_b[:, lo:hi], MULT
                 )
             for lo, hi in ((0, 256), (256, 512)):
                 nc.vector.tensor_tensor(
@@ -168,10 +168,16 @@ def tile_list_rink_loop_features_kernel(
                 )
 
         def weave_scalar(a, lo, hi):
-            nc.scalar.copy(x_bf[a][:, lo:hi, :], x_raw[a][:, :, lo:hi].rearrange("p t m -> p m t"))
+            nc.scalar.copy(
+                x_bf[a][:, lo:hi, :].rearrange("p (c i) t -> p c t i", i=4),
+                x_raw[a][:, :, lo:hi].rearrange("p t (c i) -> p c t i", i=4),
+            )
 
         def weave_vector(a, lo, hi):
-            nc.vector.tensor_copy(x_bf[a][:, lo:hi, :], x_raw[a][:, :, lo:hi].rearrange("p t m -> p m t"))
+            nc.vector.tensor_copy(
+                x_bf[a][:, lo:hi, :].rearrange("p (c i) t -> p c t i", i=4),
+                x_raw[a][:, :, lo:hi].rearrange("p t (c i) -> p c t i", i=4),
+            )
 
         def quant_x(a, lo, hi):
             nc.vector.quantize_mx(
@@ -189,23 +195,20 @@ def tile_list_rink_loop_features_kernel(
             else:
                 nc.scalar.activation(d[n], d[n], ACT.Square)
 
-        def damp0_vector(n):
-            nc.vector.scalar_tensor_tensor(d[n], h[n][:], gh2[:, n : n + 1], h[n][:], MULT, MULT)
-
         ybanks = {}
 
-        def second_product(n, a):
+        def second_product(n, a, lo=0, hi=L):
             g, t = divmod(n, PACK)
             if a == 0:
-                ybanks[n] = psum.tile([P, BANK], F32, name="bank%d" % n)
+                ybanks[n] = psum.tile([P, BANK], F32, name="bank%d" % ((n + 6) % 8))
             nc.tensor.matmul_mx(
-                out=ybanks[n][:],
+                out=ybanks[n][:, lo:hi],
                 lhsT=late["wy", g][:, GROUP * a + P * t : GROUP * a + P * (t + 1)].bitcast(FP8X4),
                 lhsT_scale=late["ys", g][4 * a :, P * t : P * (t + 1)],
-                rhs=x_w[a][:].bitcast(FP8X4),
-                rhs_scale=x_s[a][:],
+                rhs=x_w[a][:, lo:hi].bitcast(FP8X4),
+                rhs_scale=x_s[a][:, lo:hi],
                 start=(a == 0),
-                stop=(a == GROUPS - 1),
+                stop=(a == GROUPS - 1 and hi == L),
             )
 
         def copy_y(n):
@@ -228,14 +231,11 @@ def tile_list_rink_loop_features_kernel(
         wb_w = dealt_b[:, : 2 * H]
         bs = dealt_b[:, 2 * H :]
         cast_wa(0, 0)
-        cast_wa(0, 1)
-        cast_wa(0, 2)
         load_wa(1, 0)
         load_wa(1, 1)
-        load_wa(1, 2)
 
         def load_wy(a):
-            late["wy_raw", a] = kept("wa_raw%d" % a, [P, H], I32)
+            late["wy_raw", a] = kept(("wa_raw0", "tabs")[a], [P, H], I32)
             nc.sync.dma_start(late["wy_raw", a][:], wy_words[a].rearrange("p c i -> p (c i)").bitcast(I32))
 
         def deal(dealt, raw):
@@ -253,33 +253,36 @@ def tile_list_rink_loop_features_kernel(
             deal(wb_w.bitcast(U16)[:, cols], wb_raw[:].bitcast(U16)[:, cols])
             deal(bs[:, cols], bs_raw[:, cols])
 
-        def deal_wy(g, tag):
+        def deal_wy(g, tag, between=None):
             both = kept(tag, [P, GROUPS * GROUP + GROUP // 4], I32)
             late["wy", g] = both[:, : GROUPS * GROUP]
             late["ys", g] = both[:, GROUPS * GROUP :].bitcast(U8)
             cols = slice(GROUP * g, GROUP * (g + 1))
             for a in range(GROUPS):
                 deal_words(both[:, GROUP * a : GROUP * (a + 1)], late["wy_raw", a][:, cols])
+            if between:
+                between()
             deal(late["ys", g], ys_raw[:, cols])
 
         deal_wb(0)
-        gh_flat = gh_t[:].rearrange("p a t -> p (a t)")
-        nc.gpsimd.tensor_tensor(gh2[:], gh_flat, gh_flat, MULT)
+        cast_wa(0, 1, nc.vector.tensor_copy)
         quant_wa(0, 0)
         first_products(0, 0)
         quant_wa(0, 1)
         deal_wb(1)
+        yh[0] = kept("yh0", [P, L + S], F32)
+        yh[1] = kept("wa_bf0", [P, L + S], F32)
         copy_hb(0, 0)
         minimum(0, 0)
 
         extra = {
-            0: [lambda: cast_wa(1, 0), lambda: load_wy(0), lambda: cast_wa(1, 1), lambda: load_wy(1), lambda: cast_wa(1, 2)],
+            0: [lambda: cast_wa(1, 0), lambda: load_wy(0), lambda: cast_wa(1, 1), lambda: load_wy(1)],
             1: [lambda: damp(0, 0), lambda: damp(0, 1), lambda: quant_wa(1, 0), lambda: quant_wa(1, 1)],
             2: [lambda: damp(0, 2), lambda: damp(1, 0)],
             3: [lambda: damp(1, 1), lambda: damp(1, 2), lambda: deal_wy(0, "wa_bf1")],
-            4: [lambda: weave_scalar(0, 0, 256), lambda: weave_scalar(0, 256, 512)],
-            5: [lambda: damp(2, 0), lambda: damp(2, 1), lambda: quant_x(0, 0, 512)],
-            6: [lambda: damp(2, 2), lambda: damp(3, 0), lambda: damp(3, 1)],
+            4: [lambda: damp(2, 0), lambda: damp(2, 1)],
+            5: [lambda: weave_scalar(0, 0, 256), lambda: weave_scalar(0, 256, 512)],
+            6: [lambda: damp(2, 2), lambda: damp(3, 0), lambda: quant_x(0, 0, 512)],
             7: [],
         }
         last = TILES - 1
@@ -302,17 +305,17 @@ def tile_list_rink_loop_features_kernel(
         weave_vector(1, 256, 512)
         quant_x(1, 0, 256)
         quant_x(1, 256, 512)
-        for n in range(PACK):
+        second_product(0, 1, 0, 256)
+        second_product(0, 1, 256, 512)
+        for n in range(1, PACK):
             second_product(n, 1)
-        deal_wy(1, "x_raw1")
+        deal_wy(1, "x_raw1", lambda: nc.vector.tensor_copy(yh[0][:, 0:L], ybanks[0][:]))
         for n in range(PACK, TILES):
             second_product(n, 0)
             second_product(n, 1)
+        damp(3, 1)
         damp(3, 2)
-        d[4] = kept("x_bf1", [P, S], F32)[:]
-        damp0_vector(4)
-        rest = [(4, 1), (4, 2)] + [(n, step) for n in range(5, TILES) for step in range(3)]
-        copy_y(0)
+        rest = [(n, step) for n in range(PACK, TILES) for step in range(3)]
         for n in range(TILES):
             if n < last:
                 copy_y(n + 1)

@@ -34,7 +34,7 @@ def tile_list_rink_loop_features_kernel(
     with ExitStack() as ctx:
         keep = ctx.enter_context(tc.tile_pool(name="keep", bufs=1))
         ring = ctx.enter_context(tc.tile_pool(name="ring", bufs=2))
-        gains = ctx.enter_context(tc.tile_pool(name="gains", bufs=5))
+        gains = ctx.enter_context(tc.tile_pool(name="gains", bufs=7))
         outp = ctx.enter_context(tc.tile_pool(name="outp", bufs=6))
         psum = ctx.enter_context(tc.psum_pool(name="psum", bufs=1))
 
@@ -50,7 +50,7 @@ def tile_list_rink_loop_features_kernel(
         vw = kept("vw", [P, S], U32)
         vs = kept("vs", [P, S], U8)
         wa_raw = {}
-        wa_bf = [kept("wa_bf%d" % a, [P, PACK, P, PACK], BF16) for a in range(GROUPS)]
+        wa_bf = {0: kept("wa_bf0", [P, PACK, P, PACK], BF16)}
         wa_w = [kept("wa_w%d" % a, [P, GROUP], U32) for a in range(GROUPS)]
         wa_s = [kept("wa_s%d" % a, [P, GROUP], U8) for a in range(GROUPS)]
         wb_raw = kept("wb_raw", [P, 2 * H], U8)
@@ -60,8 +60,8 @@ def tile_list_rink_loop_features_kernel(
         gp_t = kept("gp_t", [P, GROUPS, PACK], F32)
         gh_t = kept("gh_t", [P, GROUPS, PACK], F32)
         h = [kept("h%d" % n, [P, S], F32) for n in range(TILES)]
-        yh = {n: kept("yh%d" % n, [P, L + S], F32) for n in range(2, TILES)}
-        x_raw = [kept("x_raw%d" % a, [P, PACK, L], F32) for a in range(GROUPS)]
+        yh = {n: kept("yh%d" % n, [P, S + 16], F32) for n in range(1, TILES)}
+        x_raw = {0: kept("x_raw0", [P, PACK, L], F32)}
         d = {n: kept("d%d" % n, [P, S], F32)[:] for n in range(TILES)}
         x_bf = [kept("x_bf%d" % a, [P, L, PACK], BF16) for a in range(GROUPS)]
         x_w = [kept("x_w%d" % a, [P, L], U32) for a in range(GROUPS)]
@@ -70,6 +70,8 @@ def tile_list_rink_loop_features_kernel(
 
         nc.vector.memset(warm[:], 1.0)
         nc.vector.memset(ys_raw[:].bitcast(I32), 0)
+        for n in range(1, TILES):
+            nc.vector.memset(yh[n][:, S:], 0.0)
         nc.scalar.activation(warm[:, 0:1], warm[:, 1:2], ACT.Abs_reciprocal_sqrt)
 
         def load_plane(queue, plane, rows):
@@ -84,7 +86,7 @@ def tile_list_rink_loop_features_kernel(
 
         def load_wa(a, u):
             lo, hi = WA_PIECES[u]
-            tag = {(0, 0): "wa_raw0", (0, 1): "yh0", (1, 0): "wa_raw0", (1, 1): "tabs"}[a, u]
+            tag = {(0, 0): "wa_raw0", (0, 1): "x_raw1", (1, 0): "wa_raw0", (1, 1): "tabs"}[a, u]
             wa_raw[a, u] = kept(tag, [P, PACK, hi - lo], F32)
             nc.sync.dma_start(wa_raw[a, u][:], wa_v[:, :, GROUP * a + lo : GROUP * a + hi])
 
@@ -146,26 +148,47 @@ def tile_list_rink_loop_features_kernel(
             )
             banks[n, u] = (pa, pb)
 
+        def staged(n, u):
+            if u == 1:
+                return yh[n][:, L : L + BANK]
+            a, t = divmod((n - 1) % TILES, PACK)
+            return x_raw[a][:, t, :]
+
         def copy_hb(n, u):
-            nc.scalar.copy(yh[n][:, L + BANK * u : L + BANK * (u + 1)], banks[n, u][1][:])
+            nc.scalar.copy(staged(n, u), banks[n, u][1][:])
 
         def minimum(n, u):
             js = slice(BANK * u, BANK * (u + 1))
-            nc.vector.tensor_tensor(h[n][:, js], banks[n, u][0][:], yh[n][:, L + BANK * u : L + BANK * (u + 1)], MIN)
+            nc.vector.tensor_tensor(h[n][:, js], banks[n, u][0][:], staged(n, u), MIN)
 
-        def picks(n):
+        firsts = {}
+
+        def pick1(n, cuts):
             a, t = divmod(n, PACK)
-            gp_b = gains.tile([P, L], F32, name="gp_b")
+            gp_b = kept("wa_bf1", [P, L], F32) if n == 0 else gains.tile([P, L], F32, name="gp_b")
             nc.scalar.copy(gp_b[:], gp_t[:, a, t : t + 1].to_broadcast([P, L]))
-            g1 = ring.tile([P, L], F32, name="g1")
-            for lo, hi in ((0, 256), (256, 512)):
+            firsts[n] = ring.tile([P, L], F32, name="g1")
+            for lo, hi in zip(cuts, cuts[1:]):
                 nc.vector.tensor_tensor(
-                    g1[:, lo:hi], h[n][:].indirect(pos1_t[:, lo // 16 : hi // 16]), gp_b[:, lo:hi], MULT
+                    firsts[n][:, lo:hi], h[n][:].indirect(pos1_t[:, lo // 16 : hi // 16]), gp_b[:, lo:hi], MULT
                 )
-            for lo, hi in ((0, 256), (256, 512)):
+
+        def pick2(n, cuts):
+            a, t = divmod(n, PACK)
+            for lo, hi in zip(cuts, cuts[1:]):
                 nc.vector.tensor_tensor(
-                    x_raw[a][:, t, lo:hi], h[n][:].indirect(pos2_t[:, lo // 16 : hi // 16]), g1[:, lo:hi], MULT
+                    x_raw[a][:, t, lo:hi], h[n][:].indirect(pos2_t[:, lo // 16 : hi // 16]), firsts[n][:, lo:hi], MULT
                 )
+
+        def products(n):
+            for u in range(2):
+                first_products(n, u)
+
+        def features(n):
+            for u in range(2):
+                copy_hb(n, u)
+            for u in range(2):
+                minimum(n, u)
 
         def weave_scalar(a, lo, hi):
             nc.scalar.copy(
@@ -267,13 +290,16 @@ def tile_list_rink_loop_features_kernel(
         deal_wb(0)
         cast_wa(0, 1, nc.vector.tensor_copy)
         quant_wa(0, 0)
-        first_products(0, 0)
+        products(0)
         quant_wa(0, 1)
         deal_wb(1)
-        yh[0] = kept("yh0", [P, L + S], F32)
-        yh[1] = kept("wa_bf0", [P, L + S], F32)
-        copy_hb(0, 0)
-        minimum(0, 0)
+        yh[0] = kept("wa_bf0", [P, S + 16], F32)
+        nc.vector.memset(yh[0][:, S:], 0.0)
+        x_raw[1] = kept("x_raw1", [P, PACK, L], F32)
+        last = TILES - 1
+        features(0)
+        pick1(0, (0, L))
+        wa_bf[1] = kept("wa_bf1", [P, PACK, P, PACK], BF16)
 
         extra = {
             0: [lambda: cast_wa(1, 0), lambda: load_wy(0), lambda: cast_wa(1, 1), lambda: load_wy(1)],
@@ -283,22 +309,15 @@ def tile_list_rink_loop_features_kernel(
             4: [lambda: damp(2, 0), lambda: damp(2, 1)],
             5: [lambda: weave_scalar(0, 0, 256), lambda: weave_scalar(0, 256, 512)],
             6: [lambda: damp(2, 2), lambda: damp(3, 0), lambda: quant_x(0, 0, 512)],
-            7: [],
         }
-        last = TILES - 1
-        for n in range(TILES):
-            first_products(n, 1)
-            if n < last:
-                first_products(n + 1, 0)
-            copy_hb(n, 1)
-            if n < last:
-                copy_hb(n + 1, 0)
-            minimum(n, 1)
-            if n < last:
-                minimum(n + 1, 0)
-            picks(n)
+        for n in range(last):
+            products(n + 1)
+            features(n + 1)
+            pick2(n, (0, L))
+            pick1(n + 1, (0, L) if n + 1 < last else (0, 256, L))
             for f in extra[n]:
                 f()
+        pick2(last, (0, 256, L))
         weave_scalar(1, 0, 256)
         for n in range(PACK):
             second_product(n, 0)

from contextlib import ExitStack

import concourse.mybir as mybir

K, H, T, S, L = 512, 1024, 2048, 1024, 512
FLOPS = 2 * (2 * K * H * S + H * H * L)

F32 = mybir.dt.float32
BF16 = mybir.dt.bfloat16
I32 = mybir.dt.int32
U32 = mybir.dt.uint32
U16 = mybir.dt.uint16
U8 = mybir.dt.uint8
FP8X4 = mybir.dt.float8_e4m3fn_x4
FP4X4 = mybir.dt.float4_e2m1fn_x4
MULT = mybir.AluOpType.mult
MIN = mybir.AluOpType.min
ACT = mybir.ActivationFunctionType

P = 128
PACK = 4
GROUP = P * PACK
GROUPS = H // GROUP
TILES = H // P
BANK = 512
WA_PIECES = ((0, 320), (320, 512))
LAST_PIECES = (0, 512, 768, 896, 1024)


def tile_list_rink_loop_features_kernel(
    tc, tab_words, tab_scales, offs, pos1, pos2, pos3, wa, wb_words, wb_scales, gp, wy_words, wy_scales, gh, out
):
    nc = tc.nc
    with ExitStack() as ctx:
        keep = ctx.enter_context(tc.tile_pool(name="keep", bufs=1))
        ring = ctx.enter_context(tc.tile_pool(name="ring", bufs=2))
        gains = ctx.enter_context(tc.tile_pool(name="gains", bufs=7))
        outp = ctx.enter_context(tc.tile_pool(name="outp", bufs=6))
        psum = ctx.enter_context(tc.psum_pool(name="psum", bufs=1))

        def kept(name, shape, dtype):
            return keep.tile(shape, dtype, name=name, align_bytes=64)

        offs_t = kept("offs_t", [P, S // 16], U16)
        pos1_t = kept("pos1_t", [P, L // 16], U16)
        pos2_t = kept("pos2_t", [P, L // 16], U16)
        pos3_t = kept("pos3_t", [P, S // 16], U16)
        tabw = kept("tabw", [P, T], I32)
        tabs = kept("tabs", [P, T], U8)
        vw = kept("vw", [P, S], U32)
        vs = kept("vs", [P, S], U8)
        wa_raw = {}
        wa_bf = {0: kept("wa_bf0", [P, PACK, P, PACK], BF16)}
        wa_w = [kept("wa_w%d" % a, [P, GROUP], U32) for a in range(GROUPS)]
        wa_s = [kept("wa_s%d" % a, [P, GROUP], U8) for a in range(GROUPS)]
        wb_raw = kept("wb_raw", [P, 2 * H], U8)
        bs_raw = kept("bs_raw", [P, H], U8)
        ys_raw = kept("ys_raw", [P, H], U8)
        late = {}
        gp_t = kept("gp_t", [P, GROUPS, PACK], F32)
        gh_t = kept("gh_t", [P, GROUPS, PACK], F32)
        h = [kept("h%d" % n, [P, S], F32) for n in range(TILES)]
        yh = {n: kept("yh%d" % n, [P, S + 16], F32) for n in range(1, TILES)}
        x_raw = {0: kept("x_raw0", [P, PACK, L], F32)}
        d = {n: kept("d%d" % n, [P, S], F32)[:] for n in range(TILES)}
        x_bf = [kept("x_bf%d" % a, [P, L, PACK], BF16) for a in range(GROUPS)]
        x_w = [kept("x_w%d" % a, [P, L], U32) for a in range(GROUPS)]
        x_s = [kept("x_s%d" % a, [P, L], U8) for a in range(GROUPS)]
        warm = kept("warm", [P, 8], F32)

        nc.vector.memset(warm[:], 1.0)
        nc.vector.memset(ys_raw[:].bitcast(I32), 0)
        for n in range(1, TILES):
            nc.vector.memset(yh[n][:, S:], 0.0)
        nc.scalar.activation(warm[:, 0:1], warm[:, 1:2], ACT.Abs_reciprocal_sqrt)

        def load_plane(queue, plane, rows):
            words = rows.shape[1] // 4
            for q in range(4):
                queue.dma_start(
                    plane[32 * q : 32 * q + 32, :].bitcast(I32),
                    rows[4 * q : 4 * q + 4, :].bitcast(I32).unsqueeze(0).to_broadcast([8, 4, words]),
                )

        wa_v = wa.rearrange("(p j) c -> p j c", j=PACK)

        def load_wa(a, u):
            lo, hi = WA_PIECES[u]
            tag = {(0, 0): "wa_raw0", (0, 1): "x_raw1", (1, 0): "wa_raw0", (1, 1): "tabs"}[a, u]
            wa_raw[a, u] = kept(tag, [P, PACK, hi - lo], F32)
            nc.sync.dma_start(wa_raw[a, u][:], wa_v[:, :, GROUP * a + lo : GROUP * a + hi])

        nc.sync.dma_start(offs_t[:], offs)
        nc.sync.dma_start(gp_t[:], gp.rearrange("(a p t) -> p a t", p=P, t=PACK))
        load_plane(nc.sync, tabs, tab_scales[0])
        nc.sync.dma_start(tabw[:], tab_words[0].rearrange("p t i -> p (t i)").bitcast(I32))
        load_wa(0, 0)
        nc.sync.dma_start(wb_raw[:].bitcast(I32), wb_words[0].bitcast(I32))
        load_plane(nc.sync, bs_raw, wb_scales[0])
        load_wa(0, 1)
        nc.sync.dma_start(pos1_t[:], pos1)
        nc.sync.dma_start(pos2_t[:], pos2)
        nc.sync.dma_start(gh_t[:], gh.rearrange("(a p t) -> p a t", p=P, t=PACK))
        nc.sync.dma_start(pos3_t[:], pos3)
        for q in range(4):
            nc.sync.dma_start(ys_raw[32 * q : 32 * q + 8, :].bitcast(I32), wy_scales[:, 4 * q : 4 * q + 4, :].bitcast(I32))

        def cast_wa(a, u, copy=nc.scalar.copy):
            lo, hi = WA_PIECES[u]
            copy(
                wa_bf[a][:, :, lo // PACK : hi // PACK, :].rearrange("p t m j -> p m j t"),
                wa_raw[a, u][:].rearrange("p j (m t) -> p m j t", t=PACK),
            )

        def quant_wa(a, u):
            cols = slice(2 * P * u, 2 * P * (u + 1))
            nc.vector.quantize_mx(
                out=wa_w[a][:, cols].bitcast(FP8X4),
                scales=wa_s[a][:, cols],
                in_=wa_bf[a][:, 2 * u : 2 * u + 2].rearrange("p t m j -> p (t m j)"),
            )

        banks = {}

        def first_products(n, u):
            a, t = divmod(n, PACK)
            cols = slice(P * t, P * (t + 1))
            js = slice(BANK * u, BANK * (u + 1))
            pb = psum.tile([P, BANK], F32, name="bank%d" % u)
            nc.tensor.matmul_mx(
                out=pb[:],
                lhsT=wb_w[:, 2 * P * n : 2 * P * (n + 1)].bitcast(FP4X4),
                lhsT_scale=bs[:, P * n : P * (n + 1)],
                rhs=vw[:, js].bitcast(FP8X4),
                rhs_scale=vs[:, js],
                start=True,
                stop=True,
            )
            pa = psum.tile([P, BANK], F32, name="bank%d" % (2 + (2 * n + u) % 4))
            nc.tensor.matmul_mx(
                out=pa[:],
                lhsT=wa_w[a][:, cols].bitcast(FP8X4),
                lhsT_scale=wa_s[a][:, cols],
                rhs=vw[:, js].bitcast(FP8X4),
                rhs_scale=vs[:, js],
                start=True,
                stop=True,
            )
            banks[n, u] = (pa, pb)

        def staged(n, u):
            if u == 1:
                return yh[n][:, L : L + BANK]
            a, t = divmod((n - 1) % TILES, PACK)
            return x_raw[a][:, t, :]

        def copy_hb(n, u):
            nc.scalar.copy(staged(n, u), banks[n, u][1][:])

        def minimum(n, u):
            js = slice(BANK * u, BANK * (u + 1))
            nc.vector.tensor_tensor(h[n][:, js], banks[n, u][0][:], staged(n, u), MIN)

        firsts = {}

        def pick1(n, cuts):
            a, t = divmod(n, PACK)
            gp_b = kept("wa_bf1", [P, L], F32) if n == 0 else gains.tile([P, L], F32, name="gp_b")
            nc.scalar.copy(gp_b[:], gp_t[:, a, t : t + 1].to_broadcast([P, L]))
            firsts[n] = ring.tile([P, L], F32, name="g1")
            for lo, hi in zip(cuts, cuts[1:]):
                nc.vector.tensor_tensor(
                    firsts[n][:, lo:hi], h[n][:].indirect(pos1_t[:, lo // 16 : hi // 16]), gp_b[:, lo:hi], MULT
                )

        def pick2(n, cuts):
            a, t = divmod(n, PACK)
            for lo, hi in zip(cuts, cuts[1:]):
                nc.vector.tensor_tensor(
                    x_raw[a][:, t, lo:hi], h[n][:].indirect(pos2_t[:, lo // 16 : hi // 16]), firsts[n][:, lo:hi], MULT
                )

        def products(n):
            for u in range(2):
                first_products(n, u)

        def features(n):
            for u in range(2):
                copy_hb(n, u)
            for u in range(2):
                minimum(n, u)

        def weave_scalar(a, lo, hi):
            nc.scalar.copy(
                x_bf[a][:, lo:hi, :].rearrange("p (c i) t -> p c t i", i=4),
                x_raw[a][:, :, lo:hi].rearrange("p t (c i) -> p c t i", i=4),
            )

        def weave_vector(a, lo, hi):
            nc.vector.tensor_copy(
                x_bf[a][:, lo:hi, :].rearrange("p (c i) t -> p c t i", i=4),
                x_raw[a][:, :, lo:hi].rearrange("p t (c i) -> p c t i", i=4),
            )

        def quant_x(a, lo, hi):
            nc.vector.quantize_mx(
                out=x_w[a][:, lo:hi].bitcast(FP8X4),
                scales=x_s[a][:, lo:hi],
                in_=x_bf[a][:, lo:hi, :].rearrange("p m t -> p (m t)"),
            )

        def damp(n, step):
            a, t = divmod(n, PACK)
            if step == 0:
                nc.scalar.activation(d[n], h[n][:], ACT.Square, scale=gh_t[:, a, t : t + 1])
            elif step == 1:
                nc.scalar.activation(d[n], d[n], ACT.Abs_reciprocal_sqrt, bias=1.0)
            else:
                nc.scalar.activation(d[n], d[n], ACT.Square)

        ybanks = {}

        def second_product(n, a, lo=0, hi=L):
            g, t = divmod(n, PACK)
            if a == 0:
                ybanks[n] = psum.tile([P, BANK], F32, name="bank%d" % ((n + 6) % 8))
            nc.tensor.matmul_mx(
                out=ybanks[n][:, lo:hi],
                lhsT=late["wy", g][:, GROUP * a + P * t : GROUP * a + P * (t + 1)].bitcast(FP8X4),
                lhsT_scale=late["ys", g][4 * a :, P * t : P * (t + 1)],
                rhs=x_w[a][:, lo:hi].bitcast(FP8X4),
                rhs_scale=x_s[a][:, lo:hi],
                start=(a == 0),
                stop=(a == GROUPS - 1 and hi == L),
            )

        def copy_y(n):
            nc.scalar.copy(yh[n][:, 0:L], ybanks[n][:])

        out_v = out.rearrange("(a p t) j -> a t p j", p=P, t=PACK)

        def finish(n, cuts):
            a, t = divmod(n, PACK)
            for lo, hi in zip(cuts, cuts[1:]):
                res = outp.tile([P, hi - lo], F32, name="res")
                nc.vector.tensor_tensor(
                    res[:], yh[n][:].indirect(pos3_t[:, lo // 16 : hi // 16]), d[n][:, lo:hi], MULT
                )
                nc.sync.dma_start(out_v[a, t, :, lo:hi], res[:])

        nc.vector.tensor_copy(vs[:], tabs[:].indirect(offs_t[:]))
        nc.vector.tensor_copy(vw[:], tabw[:].bitcast(U32).indirect(offs_t[:]))
        dealt_b = kept("tabw", [P, 3 * H], U8)
        wb_w = dealt_b[:, : 2 * H]
        bs = dealt_b[:, 2 * H :]
        cast_wa(0, 0)
        load_wa(1, 0)
        load_wa(1, 1)

        def load_wy(a):
            late["wy_raw", a] = kept(("wa_raw0", "tabs")[a], [P, H], I32)
            nc.sync.dma_start(late["wy_raw", a][:], wy_words[a].rearrange("p c i -> p (c i)").bitcast(I32))

        def deal(dealt, raw):
            nc.vector.tensor_copy(
                dealt.rearrange("p (t m) -> p t m", t=PACK), raw.rearrange("p (m t) -> p t m", t=PACK)
            )

        def deal_words(dealt, raw):
            nc.vector.tensor_copy(
                dealt.rearrange("p (t c i) -> p c t i", t=PACK, i=4), raw.rearrange("p (c i t) -> p c t i", t=PACK, i=4)
            )

        def deal_wb(a):
            cols = slice(GROUP * a, GROUP * (a + 1))
            deal(wb_w.bitcast(U16)[:, cols], wb_raw[:].bitcast(U16)[:, cols])
            deal(bs[:, cols], bs_raw[:, cols])

        def deal_wy(g, tag, between=None):
            both = kept(tag, [P, GROUPS * GROUP + GROUP // 4], I32)
            late["wy", g] = both[:, : GROUPS * GROUP]
            late["ys", g] = both[:, GROUPS * GROUP :].bitcast(U8)
            cols = slice(GROUP * g, GROUP * (g + 1))
            for a in range(GROUPS):
                deal_words(both[:, GROUP * a : GROUP * (a + 1)], late["wy_raw", a][:, cols])
            if between:
                between()
            deal(late["ys", g], ys_raw[:, cols])

        deal_wb(0)
        cast_wa(0, 1, nc.vector.tensor_copy)
        quant_wa(0, 0)
        products(0)
        quant_wa(0, 1)
        deal_wb(1)
        yh[0] = kept("wa_bf0", [P, S + 16], F32)
        nc.vector.memset(yh[0][:, S:], 0.0)
        x_raw[1] = kept("x_raw1", [P, PACK, L], F32)
        last = TILES - 1
        features(0)
        pick1(0, (0, L))
        wa_bf[1] = kept("wa_bf1", [P, PACK, P, PACK], BF16)

        extra = {
            0: [lambda: cast_wa(1, 0), lambda: load_wy(0), lambda: cast_wa(1, 1), lambda: load_wy(1)],
            1: [lambda: damp(0, 0), lambda: damp(0, 1), lambda: quant_wa(1, 0), lambda: quant_wa(1, 1)],
            2: [lambda: damp(0, 2), lambda: damp(1, 0)],
            3: [lambda: damp(1, 1), lambda: damp(1, 2), lambda: deal_wy(0, "wa_bf1")],
            4: [lambda: damp(2, 0), lambda: damp(2, 1)],
            5: [lambda: weave_scalar(0, 0, 256), lambda: weave_scalar(0, 256, 512)],
            6: [lambda: damp(2, 2), lambda: damp(3, 0), lambda: quant_x(0, 0, 512)],
        }
        for n in range(last):
            products(n + 1)
            features(n + 1)
            pick2(n, (0, L))
            pick1(n + 1, (0, L) if n + 1 < last else (0, 256, L))
            for f in extra[n]:
                f()
        pick2(last, (0, 256, L))
        weave_scalar(1, 0, 256)
        for n in range(PACK):
            second_product(n, 0)
        weave_vector(1, 256, 512)
        quant_x(1, 0, 256)
        quant_x(1, 256, 512)
        second_product(0, 1, 0, 256)
        second_product(0, 1, 256, 512)
        for n in range(1, PACK):
            second_product(n, 1)
        deal_wy(1, "x_raw1", lambda: nc.vector.tensor_copy(yh[0][:, 0:L], ybanks[0][:]))
        for n in range(PACK, TILES):
            second_product(n, 0)
            second_product(n, 1)
        damp(3, 1)
        damp(3, 2)
        rest = [(n, step) for n in range(PACK, TILES) for step in range(3)]
        for n in range(TILES):
            if n < last:
                copy_y(n + 1)
            for item in rest[2 * n : 2 * n + 2]:
                damp(*item)
            finish(n, (0, S) if n < last else LAST_PIECES)
